import numpy as np
import ml_dtypes


def mxq(x, axis, fmt="e4m3"):
    dtype, down = {"e4m3": (ml_dtypes.float8_e4m3fn, 7), "e5m2": (ml_dtypes.float8_e5m2, 14)}[fmt]
    v = np.moveaxis(np.asarray(x, np.float32).astype(ml_dtypes.bfloat16).astype(np.float64), axis, -1)
    blocks = v.reshape(v.shape[:-1] + (-1, 32))
    amax = np.abs(blocks).max(-1, keepdims=True)
    byte = np.maximum(np.where(amax > 0, np.frexp(amax)[1] - 1 + 127, 0) - down, 1)
    scale = np.exp2(byte - 127.0)
    codes = (blocks / scale).astype(np.float32).astype(dtype).astype(np.float64)
    return np.moveaxis((codes * scale).reshape(v.shape), -1, axis)


WIDE = False


def mx_kscale(k):
    if not WIDE:
        return np.ones(k)
    levels = np.array([10, -10, 5, -5, 0])
    if k % 512:
        return np.exp2(np.random.permutation(np.resize(levels, k // 32))).repeat(32)
    a = np.empty((k // 512, 16))
    for p in range(k // 512):
        a[p, :8] = np.random.permutation(np.resize(levels, 8))
        for g in range(8):
            far = levels[np.abs(levels - a[p, g]) >= 10]
            a[p, g + 8] = far[np.random.randint(len(far))]
    return np.exp2(a.ravel()).repeat(32)


def f64(x):
    return np.asarray(x).astype(np.float64)


def striped(idx):
    return np.tile(idx.reshape(-1, 16).T, (8, 1)).astype(np.uint16)


def unstriped(offs):
    return offs[:16].T.reshape(-1).astype(np.int64)


E2M1 = np.array([0.0, 0.5, 1.0, 1.5, 2.0, 3.0, 4.0, 6.0, -0.0, -0.5, -1.0, -1.5, -2.0, -3.0, -4.0, -6.0])


def pack_weight(w, fmt):
    k, n = w.shape
    w = f64(np.asarray(w, np.float32).astype(ml_dtypes.bfloat16)).reshape(k // 32, 32, n)
    amax = np.abs(w).max(1)
    if fmt == "e4m3":
        byte = np.frexp(amax)[1] - 1 + 127 - 7
    else:
        mant, ex = np.frexp(amax / 6.0)
        byte = np.where(mant > 0.5, ex, ex - 1) + 127
    byte = np.clip(np.where(amax > 0, byte, 1), 1, 254)
    scaled = (w * np.exp2(127.0 - byte)[:, None, :]).reshape(k, n).astype(np.float32)
    by_word = np.ascontiguousarray(scaled.reshape(k // 512, 128, 4, n).transpose(0, 1, 3, 2))
    if fmt == "e4m3":
        words = by_word.astype(ml_dtypes.float8_e4m3fn).view(np.uint8)
    else:
        c = by_word.astype(ml_dtypes.float4_e2m1fn).view(np.uint8) & 0xF
        words = (c[..., 0::2] | (c[..., 1::2] << 4)).reshape(k // 512, 128, 2 * n)
    return np.ascontiguousarray(words), np.ascontiguousarray(byte.astype(np.uint8).reshape(k // 512, 16, n))


def unpack_weight(words, scales, fmt):
    g, _, n = scales.shape
    words = np.ascontiguousarray(words).reshape(g, 128, n, -1)
    if fmt == "e4m3":
        vals = words.view(ml_dtypes.float8_e4m3fn).astype(np.float64)
    else:
        nib = np.empty((g, 128, n, 4), np.uint8)
        nib[..., 0::2] = words & 0xF
        nib[..., 1::2] = words >> 4
        vals = E2M1[nib]
    vals = vals * np.repeat(np.exp2(scales.astype(np.float64) - 127.0), 8, axis=1)[..., None]
    return vals.transpose(0, 1, 3, 2).reshape(g * 512, n)


def gelu(v):
    return 0.5 * v * (1.0 + np.tanh(np.sqrt(2.0 / np.pi) * (v + 0.044715 * v**3)))


def striped8(idx):
    return np.concatenate([v.reshape(-1, 16).T for v in idx]).astype(np.uint16)


def unstriped8(offs):
    return np.stack([offs[16 * g:16 * g + 16].T.reshape(-1) for g in range(8)]).astype(np.int64)


def heads(h, wgt, idx8):
    r = np.arange(h.shape[0])
    return wgt[r // 4 % 128] * h[r[:, None], idx8[r % 512 // 64]]


def put_heads(h, wgs, idx8, t2):
    r = np.arange(h.shape[0])
    page = np.zeros((h.shape[0], t2))
    page[r[:, None], idx8[r % 512 // 64]] = wgs[r // 4 % 128] * h
    return page


K, H, N, T, S, P, T2 = 1024, 1024, 768, 2048, 512, 512, 1024

def setup_inputs():
    n = np.random.standard_normal
    s = mx_kscale(K)[:, None]
    u = mx_kscale(H)[:, None]
    d = {}
    d["tab_words"], d["tab_scales"] = pack_weight(n((K, T)) * s, "e4m3")
    d["offs"] = striped(np.random.permutation(T)[:S])
    d["offs2"] = striped8(np.stack([np.random.permutation(T2)[:S] for _ in range(8)]))
    d["offs3"] = striped8(np.stack([np.random.permutation(T2)[:P] for _ in range(8)]))
    d["w1"] = (1.3 * n((K, H)) / K**0.5 / s).astype(np.float32)
    d["gain"] = (u[:, 0] * np.exp(0.3 * n(H))).astype(np.float32)
    d["wgs"] = np.repeat(np.random.uniform(0.5, 2.0, (8, S)), 16, axis=0).astype(np.float32)
    d["wgt"] = np.repeat(np.random.uniform(0.5, 2.0, (8, P)), 16, axis=0).astype(np.float32)
    d["pig"] = (0.8 * n((H, P)) * u).astype(np.float32)
    d["w2_words"], d["w2_scales"] = pack_weight(n((H, N)) / H**0.5 / u, "e2m1")
    d["w3"] = (n((H, N)) / H**0.5 / u).astype(np.float32)
    return d

def reference(tab_words, tab_scales, offs, offs2, offs3, w1, gain, wgs, wgt, pig, w2_words, w2_scales, w3):
    v = unpack_weight(tab_words, tab_scales, "e4m3")[:, unstriped(offs)]
    h = np.tanh(mxq(f64(w1), 0, "e4m3").T @ v) * f64(gain)[:, None]
    page = put_heads(h, f64(wgs), unstriped8(offs2), T2)
    x = heads(page, f64(wgt), unstriped8(offs3))
    z = mxq(x - f64(pig), 0, "e4m3")
    y = unpack_weight(w2_words, w2_scales, "e2m1").T @ z
    e = mxq(f64(w3), 0, "e4m3").T @ z
    return y * np.tanh(e) + e

@@ -1,0 +1,297 @@
+from contextlib import ExitStack
+
+import concourse.mybir as mybir
+from concourse.masks import make_identity
+
+K, H, N, T, S, M, T2 = 1024, 1024, 768, 2048, 512, 512, 1024
+FLOPS = 2 * K * H * S + 2 * 2 * H * N * M
+
+F32 = mybir.dt.float32
+BF16 = mybir.dt.bfloat16
+I32 = mybir.dt.int32
+U32 = mybir.dt.uint32
+U16 = mybir.dt.uint16
+U8 = mybir.dt.uint8
+FP8X4 = mybir.dt.float8_e4m3fn_x4
+FP4X4 = mybir.dt.float4_e2m1fn_x4
+MULT = mybir.AluOpType.mult
+ADD = mybir.AluOpType.add
+TANH = mybir.ActivationFunctionType.Tanh
+COPY = mybir.ActivationFunctionType.Copy
+
+P = 128
+HALF = 256
+
+
+def tile_list_iris_ring_matcher_kernel(
+    tc, tab_words, tab_scales, offs, offs2, offs3, w1, gain, wgs, wgt, pig, w2_words, w2_scales, w3, out
+):
+    nc = tc.nc
+    with ExitStack() as ctx:
+        keep = ctx.enter_context(tc.tile_pool(name="keep", bufs=1))
+        ring = ctx.enter_context(tc.tile_pool(name="ring", bufs=2))
+        psum = ctx.enter_context(tc.psum_pool(name="psum", bufs=2))
+
+        def kept(shape, dtype, name, tag=None):
+            return keep.tile(shape, dtype, name=name, tag=tag or name, align_bytes=64)
+
+        tab_s = kept([P, T], U8, "tab_s")
+        nc.gpsimd.memset(tab_s[:].bitcast(I32), 0)
+        pages = [kept([P, T2], F32, "page%d" % i) for i in range(4)]
+        for page in pages:
+            nc.vector.memset(page[:], 0.0)
+        w2_s = kept([P, 2, N], U8, "w2_s")
+        nc.vector.memset(w2_s[:].rearrange("p a n -> p (a n)").bitcast(I32), 0)
+
+        ident = kept([P, P], F32, "ident")
+        make_identity(nc, ident[:])
+
+        list1 = keep.tile([P, S // 16], U16, name="list1")
+        list2 = keep.tile([P, S // 16], U16, name="list2")
+        list3 = keep.tile([P, M // 16], U16, name="list3")
+        nc.sync.dma_start(list1[:], offs)
+        for q in range(4):
+            nc.sync.dma_start(
+                out=tab_s[32 * q : 32 * q + 8, :].bitcast(I32),
+                in_=tab_scales[:, 4 * q : 4 * q + 4, :].bitcast(I32),
+            )
+
+        def load_w1(b, a):
+            raw = kept([P, 4, 512], F32, "w1_raw_%d_%d" % (b, a), tag="w1_raw%d" % a)
+            rows = w1[512 * a : 512 * (a + 1), 512 * b : 512 * (b + 1)]
+            nc.sync.dma_start(out=raw[:], in_=rows.rearrange("(p j) c -> p j c", j=4))
+            return raw
+
+        def cast_w1(b, a, raw):
+            grouped = kept([P, 2048], BF16, "w1_bf_%d_%d" % (b, a), tag="w1_bf%d" % a)
+            nc.scalar.copy(
+                out=grouped[:].rearrange("p (t m j) -> p m j t", t=4, j=4),
+                in_=raw[:].rearrange("p j (m t) -> p m j t", t=4),
+            )
+            return grouped
+
+        def quantise(source, name, tag=None):
+            words = source.shape[1] // 4
+            codes = kept([P, words], U32, name + "_c", tag=tag)
+            scales = kept([P, words], U8, name + "_s")
+            nc.vector.quantize_mx(out=codes[:].bitcast(FP8X4), scales=scales[:], in_=source[:])
+            return codes, scales
+
+        w1_raw = [load_w1(0, a) for a in range(2)]
+        tab_w = []
+        for a in range(2):
+            words = kept([P, T], I32, "tab_w%d" % a)
+            nc.sync.dma_start(out=words[:], in_=tab_words[a].rearrange("p t i -> p (t i)").bitcast(I32))
+            tab_w.append(words)
+        wgs_sb = kept([P, S], F32, "wgs_sb")
+        nc.sync.dma_start(out=wgs_sb[:], in_=wgs)
+        nc.sync.dma_start(list2[:], offs2)
+        gain_sb = kept([P, 2, 4], F32, "gain_sb")
+        nc.sync.dma_start(out=gain_sb[:], in_=gain.rearrange("(b p i) -> p b i", b=2, i=4))
+
+        w1_q = {}
+        for a in range(2):
+            w1_q[0, a] = quantise(cast_w1(0, a, w1_raw[a]), "w1_0_%d" % a)
+        v_s = kept([P, S], U8, "v_s")
+        nc.vector.tensor_copy(v_s[:], tab_s[:].indirect(list1[:]))
+        v_w = [kept([P, S], U32, "v_w%d" % a) for a in range(2)]
+        nc.vector.tensor_copy(v_w[0][:], tab_w[0][:].bitcast(U32).indirect(list1[:]))
+        for hf in range(2):
+            nc.vector.tensor_copy(
+                v_w[1][:, HALF * hf : HALF * (hf + 1)],
+                tab_w[1][:].bitcast(U32).indirect(list1[:, 16 * hf : 16 * (hf + 1)]),
+            )
+
+        w1_raw = [load_w1(1, a) for a in range(2)]
+        wgt_sb = kept([P, M], F32, "wgt_sb")
+        nc.sync.dma_start(out=wgt_sb[:], in_=wgt)
+        nc.sync.dma_start(list3[:], offs3)
+        pig_sb = [kept([P, 4, M], F32, "pig%d" % b) for b in range(2)]
+        nc.sync.dma_start(out=pig_sb[0][:], in_=pig[0:512, :].rearrange("(p i) m -> p i m", i=4))
+        w3_raw = [kept([P, 4, N], F32, "w3_raw%d" % a) for a in range(2)]
+        for a in range(2):
+            nc.sync.dma_start(
+                out=w3_raw[a][:], in_=w3[512 * a : 512 * (a + 1), :].rearrange("(p j) n -> p j n", j=4)
+            )
+        nc.sync.dma_start(out=pig_sb[1][:], in_=pig[512:1024, :].rearrange("(p i) m -> p i m", i=4))
+        w2_w = kept([P, 2, 2 * N], U8, "w2_w")
+        nc.sync.dma_start(out=w2_w[:].bitcast(I32), in_=w2_words.rearrange("a p c -> p a c").bitcast(I32))
+        for q in range(4):
+            nc.sync.dma_start(
+                out=w2_s[32 * q : 32 * q + 4, :, :].bitcast(I32),
+                in_=w2_scales[:, 4 * q : 4 * q + 4, :].rearrange("a r n -> r a n").bitcast(I32),
+            )
+
+        def gained(s):
+            weight = kept([P, S], F32, "wg%d" % s)
+            column = gain_sb[:, s // 4, s % 4 : s % 4 + 1]
+            if s == 0:
+                nc.vector.tensor_scalar(weight[:], wgs_sb[:], column, None, MULT)
+            else:
+                nc.scalar.activation(weight[:], wgs_sb[:], COPY, scale=column)
+            return weight
+
+        def first_product(s, h, lo, hi):
+            b, i = divmod(s, 4)
+            acc = psum.tile([P, 512], F32, name="acc", tag="acc", bufs=4)
+            for a in range(2):
+                codes, scales = w1_q[b, a]
+                nc.tensor.matmul_mx(
+                    out=acc[:, 0 : hi - lo],
+                    lhsT=codes[:, P * i : P * (i + 1)].bitcast(FP8X4),
+                    lhsT_scale=scales[:, P * i : P * (i + 1)],
+                    rhs=v_w[a][:, lo:hi].bitcast(FP8X4),
+                    rhs_scale=v_s[4 * a : P, lo:hi],
+                    start=(a == 0),
+                    stop=(a == 1),
+                )
+            nc.scalar.activation(h[:, lo:hi], acc[:, 0 : hi - lo], TANH)
+
+        def put(s):
+            h = kept([P, S], F32, "h%d" % s)
+            weight = gained(s)
+            runs = [(0, HALF), (HALF, S)] if s == 0 else [(0, S)]
+            for lo, hi in runs:
+                first_product(s, h, lo, hi)
+            for lo, hi in runs:
+                nc.vector.tensor_tensor(
+                    pages[s % 4][:].indirect(list2[:, lo // 16 : hi // 16]), h[:, lo:hi], weight[:, lo:hi], MULT
+                )
+
+        x_neg = {}
+
+        def pick(s, lo, hi, tag=None):
+            if s not in x_neg:
+                x_neg[s] = kept([P, M], F32, "x%d" % s, tag=tag)
+            nc.vector.tensor_tensor(
+                x_neg[s][:, lo:hi], pages[s % 4][:].indirect(list3[:, lo // 16 : hi // 16]), wgt_neg[:, lo:hi], MULT
+            )
+
+        turned = {}
+
+        def difference(b, u, hf):
+            bank = psum.tile([P, 2, 2, P], F32, name="z_t", tag="z_t")
+            places = [(c, e) for c in range(2) for e in range(2)]
+            for term in range(2):
+                for c, e in places:
+                    cols = slice(HALF * hf + P * c, HALF * hf + P * (c + 1))
+                    source = pig_sb[b][:, 2 * u + e, cols] if term == 0 else x_neg[4 * b + 2 * u + e][:, cols]
+                    nc.tensor.matmul(
+                        bank[:, c, e, :],
+                        source,
+                        ident[:],
+                        start=(term == 0 and (c, e) == places[0]),
+                        stop=(term == 1 and (c, e) == places[-1]),
+                        is_transpose=True,
+                    )
+            pairs = ring.tile([P, 2 * P * 2], BF16, name="pairs")
+            nc.scalar.activation(
+                pairs[:].rearrange("m (c p e) -> m c p e", c=2, e=2),
+                bank[:].rearrange("m c e p -> m c p e"),
+                COPY,
+                scale=-1.0,
+            )
+            if (b, hf) not in turned:
+                turned[b, hf] = psum.tile([P, 2, HALF], F32, name="z_w", tag="z_w")
+            for c in range(2):
+                nc.tensor.transpose(
+                    turned[b, hf][:, u, P * c : P * (c + 1)], pairs[:].bitcast(F32)[:, P * c : P * (c + 1)], ident[:]
+                )
+
+        z_q = {}
+
+        def quantise_z(b, hf, tag=None):
+            grouped = kept([P, 4 * HALF], BF16, "z_bf_%d_%d" % (b, hf), tag=tag)
+            nc.scalar.copy(
+                out=grouped[:].bitcast(F32).rearrange("p (m u) -> p m u", u=2),
+                in_=turned[b, hf][:].rearrange("p u m -> p m u"),
+            )
+            z_q[b, hf] = quantise(grouped, "z_%d_%d" % (b, hf))
+
+        for s in range(4):
+            put(s)
+        w1_bf = [cast_w1(1, a, w1_raw[a]) for a in range(2)]
+        wgt_neg = kept([P, M], F32, "wgt_neg")
+        nc.scalar.activation(wgt_neg[:], wgt_sb[:], COPY, scale=-1.0)
+        pick(0, 0, M)
+        pick(1, 0, M)
+        for a in range(2):
+            w1_q[1, a] = quantise(w1_bf[a], "w1_1_%d" % a)
+        pick(2, 0, M, tag="w1_bf1")
+        pick(3, 0, M)
+        for s in range(4, 8):
+            put(s)
+        for u in range(2):
+            for hf in range(2):
+                difference(0, u, hf)
+        for hf in range(2):
+            quantise_z(0, hf)
+
+        w3_bf = [kept([P, 2, HALF * 4], BF16, "w3_bf%d" % k) for k in range(3)]
+        for k in range(3):
+            for a in range(2):
+                nc.scalar.copy(
+                    out=w3_bf[k][:, a, :].rearrange("p (c i j) -> p c j i", i=4, j=4),
+                    in_=w3_raw[a][:, :, HALF * k : HALF * (k + 1)].rearrange("p j (c i) -> p c j i", i=4),
+                )
+
+        for hf in range(2):
+            for s in range(4, 8):
+                pick(s, HALF * hf, HALF * (hf + 1))
+        for u in range(2):
+            difference(1, u, 0)
+        quantise_z(1, 0, tag="late")
+        w3_c = kept([P, 3, 512], U32, "w3_c", tag="late")
+        w3_s = [kept([P, 512], U8, "w3_s%d" % k) for k in range(3)]
+        for k in range(3):
+            nc.vector.quantize_mx(
+                out=w3_c[:, k, :].bitcast(FP8X4), scales=w3_s[k][:], in_=w3_bf[k][:].rearrange("p a c -> p (a c)")
+            )
+        for u in range(2):
+            difference(1, u, 1)
+
+        def finish(hf, k):
+            y = psum.tile([P, 2, HALF], F32, name="y", tag="acc", bufs=4)
+            for j in range(2):
+                n0 = HALF * k + P * j
+                for m0 in range(0, HALF, P):
+                    for a in range(2):
+                        codes, scales = z_q[a, hf]
+                        nc.tensor.matmul_mx(
+                            out=y[:, j, m0 : m0 + P],
+                            lhsT=w2_w[:, a, 2 * n0 : 2 * (n0 + P)].bitcast(FP4X4),
+                            lhsT_scale=w2_s[:, a, n0 : n0 + P],
+                            rhs=codes[:, m0 : m0 + P].bitcast(FP8X4),
+                            rhs_scale=scales[:, m0 : m0 + P],
+                            start=(a == 0),
+                            stop=(a == 1),
+                        )
+            e = psum.tile([P, 2, HALF], F32, name="e", tag="acc", bufs=4)
+            for j in range(2):
+                for a in range(2):
+                    codes, scales = z_q[a, hf]
+                    cols = slice(HALF * a + P * j, HALF * a + P * (j + 1))
+                    nc.tensor.matmul_mx(
+                        out=e[:, j, :],
+                        lhsT=w3_c[:, k, cols].bitcast(FP8X4),
+                        lhsT_scale=w3_s[k][:, cols],
+                        rhs=codes[:].bitcast(FP8X4),
+                        rhs_scale=scales[:],
+                        start=(a == 0),
+                        stop=(a == 1),
+                    )
+            bent = ring.tile([P, 2, HALF], F32, name="bent")
+            nc.scalar.activation(bent[:], e[:], TANH)
+            gated = ring.tile([P, 2, HALF], F32, name="gated")
+            nc.vector.tensor_tensor(gated[:], y[:], bent[:], MULT)
+            result = ring.tile([P, 2, HALF], F32, name="result", bufs=4)
+            nc.vector.tensor_tensor(result[:], e[:], gated[:], ADD)
+            rows = out[HALF * k : HALF * (k + 1), HALF * hf : HALF * (hf + 1)]
+            nc.sync.dma_start(out=rows.rearrange("(j p) m -> p j m", p=P), in_=result[:])
+
+        finish(0, 0)
+        quantise_z(1, 1)
+        finish(0, 1)
+        finish(0, 2)
+        for k in range(3):
+            finish(1, k)

@@ -30,10 +30,18 @@ def tile_list_iris_ring_matcher_kernel(
     with ExitStack() as ctx:
         keep = ctx.enter_context(tc.tile_pool(name="keep", bufs=1))
         ring = ctx.enter_context(tc.tile_pool(name="ring", bufs=2))
-        psum = ctx.enter_context(tc.psum_pool(name="psum", bufs=2))
+        reuse = ctx.enter_context(tc.tile_pool(name="reuse", bufs=1))
+        psum = ctx.enter_context(tc.psum_pool(name="psum", bufs=1))
 
-        def kept(shape, dtype, name, tag=None):
+        def bank(number, shape, name):
+            return psum.tile(shape, F32, name=name, tag="bank%d" % number)
+
+        def kept(shape, dtype, name, tag=None, at=None):
+            if at is not None:
+                return reuse.tile(shape, dtype, name=name, align_bytes=64, offset=at)
             return keep.tile(shape, dtype, name=name, tag=tag or name, align_bytes=64)
+
+        WGS_AT, AFTER_Z, AFTER_PICKS, AFTER_GATE = 3008, 8192, 10240, 12288
 
         tab_s = kept([P, T], U8, "tab_s")
         nc.gpsimd.memset(tab_s[:].bitcast(I32), 0)
@@ -42,7 +50,6 @@ def tile_list_iris_ring_matcher_kernel(
             nc.vector.memset(page[:], 0.0)
         w2_s = kept([P, 2, N], U8, "w2_s")
         nc.vector.memset(w2_s[:].rearrange("p a n -> p (a n)").bitcast(I32), 0)
-
         ident = kept([P, P], F32, "ident")
         make_identity(nc, ident[:])
 
@@ -70,10 +77,10 @@ def tile_list_iris_ring_matcher_kernel(
             )
             return grouped
 
-        def quantise(source, name, tag=None):
+        def quantise(source, name, at=None):
             words = source.shape[1] // 4
-            codes = kept([P, words], U32, name + "_c", tag=tag)
-            scales = kept([P, words], U8, name + "_s")
+            codes = kept([P, words], U32, name + "_c")
+            scales = kept([P, words], U8, name + "_s", at=at)
             nc.vector.quantize_mx(out=codes[:].bitcast(FP8X4), scales=scales[:], in_=source[:])
             return codes, scales
 
@@ -83,7 +90,7 @@ def tile_list_iris_ring_matcher_kernel(
             words = kept([P, T], I32, "tab_w%d" % a)
             nc.sync.dma_start(out=words[:], in_=tab_words[a].rearrange("p t i -> p (t i)").bitcast(I32))
             tab_w.append(words)
-        wgs_sb = kept([P, S], F32, "wgs_sb")
+        wgs_sb = kept([P, S], F32, "wgs_sb", at=WGS_AT)
         nc.sync.dma_start(out=wgs_sb[:], in_=wgs)
         nc.sync.dma_start(list2[:], offs2)
         gain_sb = kept([P, 2, 4], F32, "gain_sb")
@@ -102,18 +109,21 @@ def tile_list_iris_ring_matcher_kernel(
                 tab_w[1][:].bitcast(U32).indirect(list1[:, 16 * hf : 16 * (hf + 1)]),
             )
 
-        w1_raw = [load_w1(1, a) for a in range(2)]
         wgt_sb = kept([P, M], F32, "wgt_sb")
         nc.sync.dma_start(out=wgt_sb[:], in_=wgt)
         nc.sync.dma_start(list3[:], offs3)
         pig_sb = [kept([P, 4, M], F32, "pig%d" % b) for b in range(2)]
-        nc.sync.dma_start(out=pig_sb[0][:], in_=pig[0:512, :].rearrange("(p i) m -> p i m", i=4))
         w3_raw = [kept([P, 4, N], F32, "w3_raw%d" % a) for a in range(2)]
-        for a in range(2):
-            nc.sync.dma_start(
-                out=w3_raw[a][:], in_=w3[512 * a : 512 * (a + 1), :].rearrange("(p j) n -> p j n", j=4)
-            )
-        nc.sync.dma_start(out=pig_sb[1][:], in_=pig[512:1024, :].rearrange("(p i) m -> p i m", i=4))
+
+        def load_rows(tile, source, a):
+            rows = source[512 * a : 512 * (a + 1), :]
+            nc.sync.dma_start(out=tile[:], in_=rows.rearrange("(p j) n -> p j n", j=4))
+
+        load_rows(w3_raw[0], w3, 0)
+        w1_raw = [load_w1(1, a) for a in range(2)]
+        load_rows(pig_sb[0], pig, 0)
+        load_rows(w3_raw[1], w3, 1)
+        load_rows(pig_sb[1], pig, 1)
         w2_w = kept([P, 2, 2 * N], U8, "w2_w")
         nc.sync.dma_start(out=w2_w[:].bitcast(I32), in_=w2_words.rearrange("a p c -> p a c").bitcast(I32))
         for q in range(4):
@@ -123,7 +133,7 @@ def tile_list_iris_ring_matcher_kernel(
             )
 
         def gained(s):
-            weight = kept([P, S], F32, "wg%d" % s)
+            weight = kept([P, S], F32, "wg%d" % s, tag="wg5" if s == 7 else None)
             column = gain_sb[:, s // 4, s % 4 : s % 4 + 1]
             if s == 0:
                 nc.vector.tensor_scalar(weight[:], wgs_sb[:], column, None, MULT)
@@ -133,7 +143,7 @@ def tile_list_iris_ring_matcher_kernel(
 
         def first_product(s, h, lo, hi):
             b, i = divmod(s, 4)
-            acc = psum.tile([P, 512], F32, name="acc", tag="acc", bufs=4)
+            acc = bank((s + (lo > 0 or s > 0)) % 2, [P, 512], "acc")
             for a in range(2):
                 codes, scales = w1_q[b, a]
                 nc.tensor.matmul_mx(
@@ -147,52 +157,59 @@ def tile_list_iris_ring_matcher_kernel(
                 )
             nc.scalar.activation(h[:, lo:hi], acc[:, 0 : hi - lo], TANH)
 
-        def put(s):
+        def runs_of(s):
+            return [(0, HALF), (HALF, S)] if s == 0 else [(0, S)]
+
+        def first_stage(s):
             h = kept([P, S], F32, "h%d" % s)
-            weight = gained(s)
-            runs = [(0, HALF), (HALF, S)] if s == 0 else [(0, S)]
-            for lo, hi in runs:
+            for lo, hi in runs_of(s):
                 first_product(s, h, lo, hi)
-            for lo, hi in runs:
+            return h
+
+        def scatter(s, h):
+            for lo, hi in runs_of(s):
                 nc.vector.tensor_tensor(
-                    pages[s % 4][:].indirect(list2[:, lo // 16 : hi // 16]), h[:, lo:hi], weight[:, lo:hi], MULT
+                    pages[s % 4][:].indirect(list2[:, lo // 16 : hi // 16]), h[:, lo:hi], weights[s][:, lo:hi], MULT
                 )
+
+        def put(s):
+            scatter(s, first_stage(s))
 
         x_neg = {}
 
-        def pick(s, lo, hi, tag=None):
-            if s not in x_neg:
-                x_neg[s] = kept([P, M], F32, "x%d" % s, tag=tag)
+        def pick(s, lo, hi, picked):
+            for hf in range(lo // HALF, hi // HALF):
+                x_neg[s, hf] = picked[:, HALF * hf - lo : HALF * (hf + 1) - lo]
             nc.vector.tensor_tensor(
-                x_neg[s][:, lo:hi], pages[s % 4][:].indirect(list3[:, lo // 16 : hi // 16]), wgt_neg[:, lo:hi], MULT
+                picked, pages[s % 4][:].indirect(list3[:, lo // 16 : hi // 16]), wgt_neg[:, lo:hi], MULT
             )
 
         turned = {}
 
-        def difference(b, u, hf):
-            bank = psum.tile([P, 2, 2, P], F32, name="z_t", tag="z_t")
+        def difference(b, u, hf, sum_bank, word_bank):
+            summed = bank(sum_bank, [P, 2, 2, P], "z_t")
             places = [(c, e) for c in range(2) for e in range(2)]
             for term in range(2):
                 for c, e in places:
                     cols = slice(HALF * hf + P * c, HALF * hf + P * (c + 1))
-                    source = pig_sb[b][:, 2 * u + e, cols] if term == 0 else x_neg[4 * b + 2 * u + e][:, cols]
+                    source = pig_sb[b][:, 2 * u + e, cols] if term == 0 else x_neg[4 * b + 2 * u + e, hf][:, P * c : P * (c + 1)]
                     nc.tensor.matmul(
-                        bank[:, c, e, :],
+                        summed[:, c, e, :],
                         source,
                         ident[:],
                         start=(term == 0 and (c, e) == places[0]),
                         stop=(term == 1 and (c, e) == places[-1]),
                         is_transpose=True,
                     )
-            pairs = ring.tile([P, 2 * P * 2], BF16, name="pairs")
+            pairs = kept([P, 2 * P * 2], BF16, "pairs")
             nc.scalar.activation(
                 pairs[:].rearrange("m (c p e) -> m c p e", c=2, e=2),
-                bank[:].rearrange("m c e p -> m c p e"),
+                summed[:].rearrange("m c e p -> m c p e"),
                 COPY,
                 scale=-1.0,
             )
             if (b, hf) not in turned:
-                turned[b, hf] = psum.tile([P, 2, HALF], F32, name="z_w", tag="z_w")
+                turned[b, hf] = bank(word_bank, [P, 2, HALF], "z_w")
             for c in range(2):
                 nc.tensor.transpose(
                     turned[b, hf][:, u, P * c : P * (c + 1)], pairs[:].bitcast(F32)[:, P * c : P * (c + 1)], ident[:]
@@ -200,98 +217,169 @@ def tile_list_iris_ring_matcher_kernel(
 
         z_q = {}
 
-        def quantise_z(b, hf, tag=None):
-            grouped = kept([P, 4 * HALF], BF16, "z_bf_%d_%d" % (b, hf), tag=tag)
+        def interleave_z(b, hf, at=None):
+            grouped = kept([P, 4 * HALF], BF16, "z_bf_%d_%d" % (b, hf), at=at)
             nc.scalar.copy(
                 out=grouped[:].bitcast(F32).rearrange("p (m u) -> p m u", u=2),
                 in_=turned[b, hf][:].rearrange("p u m -> p m u"),
             )
-            z_q[b, hf] = quantise(grouped, "z_%d_%d" % (b, hf))
+            return grouped
 
-        for s in range(4):
-            put(s)
-        w1_bf = [cast_w1(1, a, w1_raw[a]) for a in range(2)]
-        wgt_neg = kept([P, M], F32, "wgt_neg")
-        nc.scalar.activation(wgt_neg[:], wgt_sb[:], COPY, scale=-1.0)
-        pick(0, 0, M)
-        pick(1, 0, M)
-        for a in range(2):
-            w1_q[1, a] = quantise(w1_bf[a], "w1_1_%d" % a)
-        pick(2, 0, M, tag="w1_bf1")
-        pick(3, 0, M)
-        for s in range(4, 8):
-            put(s)
-        for u in range(2):
-            for hf in range(2):
-                difference(0, u, hf)
-        for hf in range(2):
-            quantise_z(0, hf)
+        w3_bf = [kept([P, 2 * HALF * 4], BF16, "w3_bf%d" % k) for k in range(3)]
 
-        w3_bf = [kept([P, 2, HALF * 4], BF16, "w3_bf%d" % k) for k in range(3)]
-        for k in range(3):
-            for a in range(2):
+        def cast_w3(a):
+            for k in range(3):
                 nc.scalar.copy(
-                    out=w3_bf[k][:, a, :].rearrange("p (c i j) -> p c j i", i=4, j=4),
+                    out=w3_bf[k][:, 4 * HALF * a : 4 * HALF * (a + 1)].rearrange("p (c i j) -> p c j i", i=4, j=4),
                     in_=w3_raw[a][:, :, HALF * k : HALF * (k + 1)].rearrange("p j (c i) -> p c j i", i=4),
                 )
 
-        for hf in range(2):
-            for s in range(4, 8):
-                pick(s, HALF * hf, HALF * (hf + 1))
-        for u in range(2):
-            difference(1, u, 0)
-        quantise_z(1, 0, tag="late")
-        w3_c = kept([P, 3, 512], U32, "w3_c", tag="late")
-        w3_s = [kept([P, 512], U8, "w3_s%d" % k) for k in range(3)]
-        for k in range(3):
-            nc.vector.quantize_mx(
-                out=w3_c[:, k, :].bitcast(FP8X4), scales=w3_s[k][:], in_=w3_bf[k][:].rearrange("p a c -> p (a c)")
-            )
-        for u in range(2):
-            difference(1, u, 1)
+        weights = {}
+        for s in range(4):
+            weights[s] = gained(s)
+            put(s)
+        wgt_neg = kept([P, M], F32, "wgt_neg", at=AFTER_PICKS)
+        nc.scalar.activation(wgt_neg[:], wgt_sb[:], COPY, scale=-1.0)
+        wgt_turned = bank(2, [P, 4, P], "wgt_turned")
+        for c in range(4):
+            nc.tensor.transpose(wgt_turned[:, c, :], wgt_sb[:, P * c : P * (c + 1)], ident[:])
+        wgt_t = kept([P, 4, 8], F32, "wgt_t")
+        nc.scalar.copy(out=wgt_t[:], in_=wgt_turned[:, :, 0:P:16])
 
-        def finish(hf, k):
-            y = psum.tile([P, 2, HALF], F32, name="y", tag="acc", bufs=4)
-            for j in range(2):
-                n0 = HALF * k + P * j
-                for m0 in range(0, HALF, P):
-                    for a in range(2):
-                        codes, scales = z_q[a, hf]
+        plain = {}
+
+        def pick_plain(first, tag):
+            both = kept([P, 2 * M], F32, "g%d" % first, tag=tag)
+            for place in range(2):
+                plain[first + place] = both[:, M * place : M * (place + 1)]
+                nc.vector.tensor_copy(plain[first + place], pages[first + place][:].indirect(list3[:]))
+
+        pick_plain(0, "g0")
+        cast_w3(0)
+        for a in range(2):
+            w1_q[1, a] = quantise(cast_w1(1, a, w1_raw[a]), "w1_1_%d" % a)
+        pick_plain(2, "w1_raw1")
+        for s in range(4, 7):
+            weights[s] = gained(s)
+        hs = {s: first_stage(s) for s in range(4, 8)}
+        for s in range(4, 7):
+            scatter(s, hs[s])
+
+        pig_t = []
+        for c in range(4):
+            turned_pig = bank(4 + c % 2, [P, 4, P], "turned_pig")
+            for i in range(4):
+                nc.tensor.transpose(turned_pig[:, i, :], pig_sb[0][:, i, P * c : P * (c + 1)], ident[:])
+            pig_t.append(kept([P, 4, P], F32, "pig_t%d" % c))
+            nc.scalar.activation(pig_t[c][:], turned_pig[:], COPY, scale=-1.0)
+
+        z_bf = [kept([P, 4 * HALF], BF16, "z_bf_0_%d" % hf) for hf in range(2)]
+
+        def weigh(c):
+            turned_g = bank(2 + c % 2, [P, 4, P], "turned_g")
+            for i in range(4):
+                nc.tensor.transpose(turned_g[:, i, :], plain[i][:, P * c : P * (c + 1)], ident[:])
+            x_t = ring.tile([P, 4, P], F32, name="x_t")
+            for g in range(8):
+                run = slice(16 * g, 16 * (g + 1))
+                nc.scalar.activation(x_t[:, :, run], turned_g[:, :, run], COPY, scale=wgt_t[:, c, g : g + 1])
+            summed = bank(6 + c % 2, [P, 4, P], "z_0")
+            for term, source in enumerate((pig_t[c], x_t)):
+                for i in range(4):
+                    nc.tensor.matmul(
+                        summed[:, i, :],
+                        source[:, i, :],
+                        ident[:],
+                        start=(term == 0 and i == 0),
+                        stop=(term == 1 and i == 3),
+                        is_transpose=True,
+                    )
+            nc.scalar.copy(
+                out=z_bf[c // 2][:, 512 * (c % 2) : 512 * (c % 2 + 1)].rearrange("p (m i) -> p m i", i=4),
+                in_=summed[:].rearrange("p i m -> p m i"),
+            )
+
+        weigh(0)
+        weigh(1)
+        weights[7] = gained(7)
+        scatter(7, hs[7])
+        weigh(2)
+        weigh(3)
+        cast_w3(1)
+
+        w3_q = {}
+        x_low = kept([P, 3 * HALF], F32, "x_low", at=0)
+        x_high = kept([P, 3 * HALF], F32, "x_high", at=WGS_AT + 2048 - 64)
+        x7_low = kept([P, HALF], F32, "x7_low")
+        for s in range(3):
+            pick(4 + s, 0, HALF, x_low[:, HALF * s : HALF * (s + 1)])
+        pick(7, 0, HALF, x7_low[:])
+        z_q[0, 0] = quantise(z_bf[0], "z_0_0", at=WGS_AT + 64)
+        w3_q[0] = quantise(w3_bf[0], "w3_0", at=WGS_AT + 64 + 256)
+        for s in range(3):
+            pick(4 + s, HALF, M, x_high[:, HALF * s : HALF * (s + 1)])
+        difference(1, 0, 0, 2, 6)
+        difference(1, 1, 0, 3, 6)
+        z_q[1, 0] = quantise(interleave_z(1, 0, at=AFTER_Z), "z_1_0")
+        x7_high = kept([P, HALF], F32, "x7_high", at=AFTER_Z)
+        pick(7, HALF, M, x7_high[:])
+        w3_q[1] = quantise(w3_bf[1], "w3_1", at=AFTER_Z + 1024)
+        w3_q[2] = quantise(w3_bf[2], "w3_2", at=AFTER_PICKS)
+        z_q[0, 1] = quantise(z_bf[1], "z_0_1", at=AFTER_PICKS + 512)
+        difference(1, 0, 1, 4, 2)
+
+        def finish(hf, k, e_bank, y_bank):
+            e = bank(e_bank, [P, 2, HALF], "e")
+            y = bank(y_bank, [P, 2, HALF], "y")
+            for a in range(2):
+                codes, scales = z_q[a, hf]
+                for j in range(2):
+                    w3_codes, w3_scales = w3_q[k]
+                    cols = slice(HALF * a + P * j, HALF * a + P * (j + 1))
+                    nc.tensor.matmul_mx(
+                        out=e[:, j, :],
+                        lhsT=w3_codes[:, cols].bitcast(FP8X4),
+                        lhsT_scale=w3_scales[:, cols],
+                        rhs=codes[:].bitcast(FP8X4),
+                        rhs_scale=scales[:],
+                        start=(a == 0 and j == 0),
+                        stop=(a == 1 and j == 1),
+                    )
+                for j in range(2):
+                    n0 = HALF * k + P * j
+                    for m0 in range(0, HALF, P):
                         nc.tensor.matmul_mx(
                             out=y[:, j, m0 : m0 + P],
                             lhsT=w2_w[:, a, 2 * n0 : 2 * (n0 + P)].bitcast(FP4X4),
                             lhsT_scale=w2_s[:, a, n0 : n0 + P],
                             rhs=codes[:, m0 : m0 + P].bitcast(FP8X4),
                             rhs_scale=scales[:, m0 : m0 + P],
-                            start=(a == 0),
-                            stop=(a == 1),
+                            start=(a == 0 and j == 0 and m0 == 0),
+                            stop=(a == 1 and j == 1 and m0 == P),
                         )
-            e = psum.tile([P, 2, HALF], F32, name="e", tag="acc", bufs=4)
-            for j in range(2):
-                for a in range(2):
-                    codes, scales = z_q[a, hf]
-                    cols = slice(HALF * a + P * j, HALF * a + P * (j + 1))
-                    nc.tensor.matmul_mx(
-                        out=e[:, j, :],
-                        lhsT=w3_c[:, k, cols].bitcast(FP8X4),
-                        lhsT_scale=w3_s[k][:, cols],
-                        rhs=codes[:].bitcast(FP8X4),
-                        rhs_scale=scales[:],
-                        start=(a == 0),
-                        stop=(a == 1),
-                    )
-            bent = ring.tile([P, 2, HALF], F32, name="bent")
+            if (hf, k) == (0, 1):
+                bent = kept([P, 2, HALF], F32, "bent_0_1", at=AFTER_GATE)
+            else:
+                bent = ring.tile([P, 2, HALF], F32, name="bent")
             nc.scalar.activation(bent[:], e[:], TANH)
             gated = ring.tile([P, 2, HALF], F32, name="gated")
-            nc.vector.tensor_tensor(gated[:], y[:], bent[:], MULT)
             result = ring.tile([P, 2, HALF], F32, name="result", bufs=4)
-            nc.vector.tensor_tensor(result[:], e[:], gated[:], ADD)
+            for j in range(2):
+                nc.vector.tensor_tensor(gated[:, j, :], y[:, j, :], bent[:, j, :], MULT)
+            for j in range(2):
+                nc.vector.tensor_tensor(result[:, j, :], e[:, j, :], gated[:, j, :], ADD)
             rows = out[HALF * k : HALF * (k + 1), HALF * hf : HALF * (hf + 1)]
-            nc.sync.dma_start(out=rows.rearrange("(j p) m -> p j m", p=P), in_=result[:])
+            if (hf, k) == (1, 2):
+                for j in range(2):
+                    nc.sync.dma_start(out=rows[P * j : P * (j + 1), :], in_=result[:, j, :])
+            else:
+                nc.sync.dma_start(out=rows.rearrange("(j p) m -> p j m", p=P), in_=result[:])
 
-        finish(0, 0)
-        quantise_z(1, 1)
-        finish(0, 1)
-        finish(0, 2)
-        for k in range(3):
-            finish(1, k)
+        finish(0, 0, 0, 1)
+        difference(1, 1, 1, 5, 2)
+        finish(0, 1, 7, 3)
+        z_q[1, 1] = quantise(interleave_z(1, 1), "z_1_1", at=AFTER_GATE)
+        finish(0, 2, 6, 4)
+        finish(1, 0, 5, 2)
+        finish(1, 1, 0, 1)
+        finish(1, 2, 7, 3)

from contextlib import ExitStack

import concourse.mybir as mybir
from concourse.masks import make_identity

K, H, N, T, S, M, T2 = 1024, 1024, 768, 2048, 512, 512, 1024
FLOPS = 2 * K * H * S + 2 * 2 * H * N * M

F32 = mybir.dt.float32
BF16 = mybir.dt.bfloat16
I32 = mybir.dt.int32
U32 = mybir.dt.uint32
U16 = mybir.dt.uint16
U8 = mybir.dt.uint8
FP8X4 = mybir.dt.float8_e4m3fn_x4
FP4X4 = mybir.dt.float4_e2m1fn_x4
MULT = mybir.AluOpType.mult
ADD = mybir.AluOpType.add
TANH = mybir.ActivationFunctionType.Tanh
COPY = mybir.ActivationFunctionType.Copy

P = 128
HALF = 256


def tile_list_iris_ring_matcher_kernel(
    tc, tab_words, tab_scales, offs, offs2, offs3, w1, gain, wgs, wgt, pig, w2_words, w2_scales, w3, out
):
    nc = tc.nc
    with ExitStack() as ctx:
        keep = ctx.enter_context(tc.tile_pool(name="keep", bufs=1))
        ring = ctx.enter_context(tc.tile_pool(name="ring", bufs=2))
        reuse = ctx.enter_context(tc.tile_pool(name="reuse", bufs=1))
        psum = ctx.enter_context(tc.psum_pool(name="psum", bufs=1))

        def bank(number, shape, name):
            return psum.tile(shape, F32, name=name, tag="bank%d" % number)

        def kept(shape, dtype, name, tag=None, at=None):
            if at is not None:
                return reuse.tile(shape, dtype, name=name, align_bytes=64, offset=at)
            return keep.tile(shape, dtype, name=name, tag=tag or name, align_bytes=64)

        WGS_AT, AFTER_Z, AFTER_PICKS, AFTER_GATE = 3008, 8192, 10240, 12288

        tab_s = kept([P, T], U8, "tab_s")
        nc.gpsimd.memset(tab_s[:].bitcast(I32), 0)
        pages = [kept([P, T2], F32, "page%d" % i) for i in range(4)]
        for page in pages:
            nc.vector.memset(page[:], 0.0)
        w2_s = kept([P, 2, N], U8, "w2_s")
        nc.vector.memset(w2_s[:].rearrange("p a n -> p (a n)").bitcast(I32), 0)
        ident = kept([P, P], F32, "ident")
        make_identity(nc, ident[:])

        list1 = keep.tile([P, S // 16], U16, name="list1")
        list2 = keep.tile([P, S // 16], U16, name="list2")
        list3 = keep.tile([P, M // 16], U16, name="list3")
        nc.sync.dma_start(list1[:], offs)
        for q in range(4):
            nc.sync.dma_start(
                out=tab_s[32 * q : 32 * q + 8, :].bitcast(I32),
                in_=tab_scales[:, 4 * q : 4 * q + 4, :].bitcast(I32),
            )

        def load_w1(b, a):
            raw = kept([P, 4, 512], F32, "w1_raw_%d_%d" % (b, a), tag="w1_raw%d" % a)
            rows = w1[512 * a : 512 * (a + 1), 512 * b : 512 * (b + 1)]
            nc.sync.dma_start(out=raw[:], in_=rows.rearrange("(p j) c -> p j c", j=4))
            return raw

        def cast_w1(b, a, raw):
            grouped = kept([P, 2048], BF16, "w1_bf_%d_%d" % (b, a), tag="w1_bf%d" % a)
            nc.scalar.copy(
                out=grouped[:].rearrange("p (t m j) -> p m j t", t=4, j=4),
                in_=raw[:].rearrange("p j (m t) -> p m j t", t=4),
            )
            return grouped

        def quantise(source, name, at=None):
            words = source.shape[1] // 4
            codes = kept([P, words], U32, name + "_c")
            scales = kept([P, words], U8, name + "_s", at=at)
            nc.vector.quantize_mx(out=codes[:].bitcast(FP8X4), scales=scales[:], in_=source[:])
            return codes, scales

        w1_raw = [load_w1(0, a) for a in range(2)]
        tab_w = []
        for a in range(2):
            words = kept([P, T], I32, "tab_w%d" % a)
            nc.sync.dma_start(out=words[:], in_=tab_words[a].rearrange("p t i -> p (t i)").bitcast(I32))
            tab_w.append(words)
        wgs_sb = kept([P, S], F32, "wgs_sb", at=WGS_AT)
        nc.sync.dma_start(out=wgs_sb[:], in_=wgs)
        nc.sync.dma_start(list2[:], offs2)
        gain_sb = kept([P, 2, 4], F32, "gain_sb")
        nc.sync.dma_start(out=gain_sb[:], in_=gain.rearrange("(b p i) -> p b i", b=2, i=4))

        w1_q = {}
        for a in range(2):
            w1_q[0, a] = quantise(cast_w1(0, a, w1_raw[a]), "w1_0_%d" % a)
        v_s = kept([P, S], U8, "v_s")
        nc.vector.tensor_copy(v_s[:], tab_s[:].indirect(list1[:]))
        v_w = [kept([P, S], U32, "v_w%d" % a) for a in range(2)]
        nc.vector.tensor_copy(v_w[0][:], tab_w[0][:].bitcast(U32).indirect(list1[:]))
        for hf in range(2):
            nc.vector.tensor_copy(
                v_w[1][:, HALF * hf : HALF * (hf + 1)],
                tab_w[1][:].bitcast(U32).indirect(list1[:, 16 * hf : 16 * (hf + 1)]),
            )

        wgt_sb = kept([P, M], F32, "wgt_sb")
        nc.sync.dma_start(out=wgt_sb[:], in_=wgt)
        nc.sync.dma_start(list3[:], offs3)
        pig_sb = [kept([P, 4, M], F32, "pig%d" % b) for b in range(2)]
        w3_raw = [kept([P, 4, N], F32, "w3_raw%d" % a) for a in range(2)]

        def load_rows(tile, source, a):
            rows = source[512 * a : 512 * (a + 1), :]
            nc.sync.dma_start(out=tile[:], in_=rows.rearrange("(p j) n -> p j n", j=4))

        load_rows(w3_raw[0], w3, 0)
        w1_raw = [load_w1(1, a) for a in range(2)]
        load_rows(pig_sb[0], pig, 0)
        load_rows(w3_raw[1], w3, 1)
        load_rows(pig_sb[1], pig, 1)
        w2_w = kept([P, 2, 2 * N], U8, "w2_w")
        nc.sync.dma_start(out=w2_w[:].bitcast(I32), in_=w2_words.rearrange("a p c -> p a c").bitcast(I32))
        for q in range(4):
            nc.sync.dma_start(
                out=w2_s[32 * q : 32 * q + 4, :, :].bitcast(I32),
                in_=w2_scales[:, 4 * q : 4 * q + 4, :].rearrange("a r n -> r a n").bitcast(I32),
            )

        def gained(s):
            weight = kept([P, S], F32, "wg%d" % s, tag="wg5" if s == 7 else None)
            column = gain_sb[:, s // 4, s % 4 : s % 4 + 1]
            if s == 0:
                nc.vector.tensor_scalar(weight[:], wgs_sb[:], column, None, MULT)
            else:
                nc.scalar.activation(weight[:], wgs_sb[:], COPY, scale=column)
            return weight

        def first_product(s, h, lo, hi):
            b, i = divmod(s, 4)
            acc = bank((s + (lo > 0 or s > 0)) % 2, [P, 512], "acc")
            for a in range(2):
                codes, scales = w1_q[b, a]
                nc.tensor.matmul_mx(
                    out=acc[:, 0 : hi - lo],
                    lhsT=codes[:, P * i : P * (i + 1)].bitcast(FP8X4),
                    lhsT_scale=scales[:, P * i : P * (i + 1)],
                    rhs=v_w[a][:, lo:hi].bitcast(FP8X4),
                    rhs_scale=v_s[4 * a : P, lo:hi],
                    start=(a == 0),
                    stop=(a == 1),
                )
            nc.scalar.activation(h[:, lo:hi], acc[:, 0 : hi - lo], TANH)

        def runs_of(s):
            return [(0, HALF), (HALF, S)] if s == 0 else [(0, S)]

        def first_stage(s):
            h = kept([P, S], F32, "h%d" % s)
            for lo, hi in runs_of(s):
                first_product(s, h, lo, hi)
            return h

        def scatter(s, h):
            for lo, hi in runs_of(s):
                nc.vector.tensor_tensor(
                    pages[s % 4][:].indirect(list2[:, lo // 16 : hi // 16]), h[:, lo:hi], weights[s][:, lo:hi], MULT
                )

        def put(s):
            scatter(s, first_stage(s))

        x_neg = {}

        def pick(s, lo, hi, picked):
            for hf in range(lo // HALF, hi // HALF):
                x_neg[s, hf] = picked[:, HALF * hf - lo : HALF * (hf + 1) - lo]
            nc.vector.tensor_tensor(
                picked, pages[s % 4][:].indirect(list3[:, lo // 16 : hi // 16]), wgt_neg[:, lo:hi], MULT
            )

        turned = {}

        def difference(b, u, hf, sum_bank, word_bank):
            summed = bank(sum_bank, [P, 2, 2, P], "z_t")
            places = [(c, e) for c in range(2) for e in range(2)]
            for term in range(2):
                for c, e in places:
                    cols = slice(HALF * hf + P * c, HALF * hf + P * (c + 1))
                    source = pig_sb[b][:, 2 * u + e, cols] if term == 0 else x_neg[4 * b + 2 * u + e, hf][:, P * c : P * (c + 1)]
                    nc.tensor.matmul(
                        summed[:, c, e, :],
                        source,
                        ident[:],
                        start=(term == 0 and (c, e) == places[0]),
                        stop=(term == 1 and (c, e) == places[-1]),
                        is_transpose=True,
                    )
            pairs = kept([P, 2 * P * 2], BF16, "pairs")
            nc.scalar.activation(
                pairs[:].rearrange("m (c p e) -> m c p e", c=2, e=2),
                summed[:].rearrange("m c e p -> m c p e"),
                COPY,
                scale=-1.0,
            )
            if (b, hf) not in turned:
                turned[b, hf] = bank(word_bank, [P, 2, HALF], "z_w")
            for c in range(2):
                nc.tensor.transpose(
                    turned[b, hf][:, u, P * c : P * (c + 1)], pairs[:].bitcast(F32)[:, P * c : P * (c + 1)], ident[:]
                )

        z_q = {}

        def interleave_z(b, hf, at=None):
            grouped = kept([P, 4 * HALF], BF16, "z_bf_%d_%d" % (b, hf), at=at)
            nc.scalar.copy(
                out=grouped[:].bitcast(F32).rearrange("p (m u) -> p m u", u=2),
                in_=turned[b, hf][:].rearrange("p u m -> p m u"),
            )
            return grouped

        w3_bf = [kept([P, 2 * HALF * 4], BF16, "w3_bf%d" % k) for k in range(3)]

        def cast_w3(a):
            for k in range(3):
                nc.scalar.copy(
                    out=w3_bf[k][:, 4 * HALF * a : 4 * HALF * (a + 1)].rearrange("p (c i j) -> p c j i", i=4, j=4),
                    in_=w3_raw[a][:, :, HALF * k : HALF * (k + 1)].rearrange("p j (c i) -> p c j i", i=4),
                )

        weights = {}
        for s in range(4):
            weights[s] = gained(s)
            put(s)
        wgt_neg = kept([P, M], F32, "wgt_neg", at=AFTER_PICKS)
        nc.scalar.activation(wgt_neg[:], wgt_sb[:], COPY, scale=-1.0)
        wgt_turned = bank(2, [P, 4, P], "wgt_turned")
        for c in range(4):
            nc.tensor.transpose(wgt_turned[:, c, :], wgt_sb[:, P * c : P * (c + 1)], ident[:])
        wgt_t = kept([P, 4, 8], F32, "wgt_t")
        nc.scalar.copy(out=wgt_t[:], in_=wgt_turned[:, :, 0:P:16])

        plain = {}

        def pick_plain(first, tag):
            both = kept([P, 2 * M], F32, "g%d" % first, tag=tag)
            for place in range(2):
                plain[first + place] = both[:, M * place : M * (place + 1)]
                nc.vector.tensor_copy(plain[first + place], pages[first + place][:].indirect(list3[:]))

        pick_plain(0, "g0")
        cast_w3(0)
        for a in range(2):
            w1_q[1, a] = quantise(cast_w1(1, a, w1_raw[a]), "w1_1_%d" % a)
        pick_plain(2, "w1_raw1")
        for s in range(4, 7):
            weights[s] = gained(s)
        hs = {s: first_stage(s) for s in range(4, 8)}
        for s in range(4, 7):
            scatter(s, hs[s])

        pig_t = []
        for c in range(4):
            turned_pig = bank(4 + c % 2, [P, 4, P], "turned_pig")
            for i in range(4):
                nc.tensor.transpose(turned_pig[:, i, :], pig_sb[0][:, i, P * c : P * (c + 1)], ident[:])
            pig_t.append(kept([P, 4, P], F32, "pig_t%d" % c))
            nc.scalar.activation(pig_t[c][:], turned_pig[:], COPY, scale=-1.0)

        z_bf = [kept([P, 4 * HALF], BF16, "z_bf_0_%d" % hf) for hf in range(2)]

        def weigh(c):
            turned_g = bank(2 + c % 2, [P, 4, P], "turned_g")
            for i in range(4):
                nc.tensor.transpose(turned_g[:, i, :], plain[i][:, P * c : P * (c + 1)], ident[:])
            x_t = ring.tile([P, 4, P], F32, name="x_t")
            for g in range(8):
                run = slice(16 * g, 16 * (g + 1))
                nc.scalar.activation(x_t[:, :, run], turned_g[:, :, run], COPY, scale=wgt_t[:, c, g : g + 1])
            summed = bank(6 + c % 2, [P, 4, P], "z_0")
            for term, source in enumerate((pig_t[c], x_t)):
                for i in range(4):
                    nc.tensor.matmul(
                        summed[:, i, :],
                        source[:, i, :],
                        ident[:],
                        start=(term == 0 and i == 0),
                        stop=(term == 1 and i == 3),
                        is_transpose=True,
                    )
            nc.scalar.copy(
                out=z_bf[c // 2][:, 512 * (c % 2) : 512 * (c % 2 + 1)].rearrange("p (m i) -> p m i", i=4),
                in_=summed[:].rearrange("p i m -> p m i"),
            )

        weigh(0)
        weigh(1)
        weights[7] = gained(7)
        scatter(7, hs[7])
        weigh(2)
        weigh(3)
        cast_w3(1)

        w3_q = {}
        x_low = kept([P, 3 * HALF], F32, "x_low", at=0)
        x_high = kept([P, 3 * HALF], F32, "x_high", at=WGS_AT + 2048 - 64)
        x7_low = kept([P, HALF], F32, "x7_low")
        for s in range(3):
            pick(4 + s, 0, HALF, x_low[:, HALF * s : HALF * (s + 1)])
        pick(7, 0, HALF, x7_low[:])
        z_q[0, 0] = quantise(z_bf[0], "z_0_0", at=WGS_AT + 64)
        w3_q[0] = quantise(w3_bf[0], "w3_0", at=WGS_AT + 64 + 256)
        for s in range(3):
            pick(4 + s, HALF, M, x_high[:, HALF * s : HALF * (s + 1)])
        difference(1, 0, 0, 2, 6)
        difference(1, 1, 0, 3, 6)
        z_q[1, 0] = quantise(interleave_z(1, 0, at=AFTER_Z), "z_1_0")
        x7_high = kept([P, HALF], F32, "x7_high", at=AFTER_Z)
        pick(7, HALF, M, x7_high[:])
        w3_q[1] = quantise(w3_bf[1], "w3_1", at=AFTER_Z + 1024)
        w3_q[2] = quantise(w3_bf[2], "w3_2", at=AFTER_PICKS)
        z_q[0, 1] = quantise(z_bf[1], "z_0_1", at=AFTER_PICKS + 512)
        difference(1, 0, 1, 4, 2)

        def finish(hf, k, e_bank, y_bank):
            e = bank(e_bank, [P, 2, HALF], "e")
            y = bank(y_bank, [P, 2, HALF], "y")
            for a in range(2):
                codes, scales = z_q[a, hf]
                for j in range(2):
                    w3_codes, w3_scales = w3_q[k]
                    cols = slice(HALF * a + P * j, HALF * a + P * (j + 1))
                    nc.tensor.matmul_mx(
                        out=e[:, j, :],
                        lhsT=w3_codes[:, cols].bitcast(FP8X4),
                        lhsT_scale=w3_scales[:, cols],
                        rhs=codes[:].bitcast(FP8X4),
                        rhs_scale=scales[:],
                        start=(a == 0 and j == 0),
                        stop=(a == 1 and j == 1),
                    )
                for j in range(2):
                    n0 = HALF * k + P * j
                    for m0 in range(0, HALF, P):
                        nc.tensor.matmul_mx(
                            out=y[:, j, m0 : m0 + P],
                            lhsT=w2_w[:, a, 2 * n0 : 2 * (n0 + P)].bitcast(FP4X4),
                            lhsT_scale=w2_s[:, a, n0 : n0 + P],
                            rhs=codes[:, m0 : m0 + P].bitcast(FP8X4),
                            rhs_scale=scales[:, m0 : m0 + P],
                            start=(a == 0 and j == 0 and m0 == 0),
                            stop=(a == 1 and j == 1 and m0 == P),
                        )
            if (hf, k) == (0, 1):
                bent = kept([P, 2, HALF], F32, "bent_0_1", at=AFTER_GATE)
            else:
                bent = ring.tile([P, 2, HALF], F32, name="bent")
            nc.scalar.activation(bent[:], e[:], TANH)
            gated = ring.tile([P, 2, HALF], F32, name="gated")
            result = ring.tile([P, 2, HALF], F32, name="result", bufs=4)
            for j in range(2):
                nc.vector.tensor_tensor(gated[:, j, :], y[:, j, :], bent[:, j, :], MULT)
            for j in range(2):
                nc.vector.tensor_tensor(result[:, j, :], e[:, j, :], gated[:, j, :], ADD)
            rows = out[HALF * k : HALF * (k + 1), HALF * hf : HALF * (hf + 1)]
            if (hf, k) == (1, 2):
                for j in range(2):
                    nc.sync.dma_start(out=rows[P * j : P * (j + 1), :], in_=result[:, j, :])
            else:
                nc.sync.dma_start(out=rows.rearrange("(j p) m -> p j m", p=P), in_=result[:])

        finish(0, 0, 0, 1)
        difference(1, 1, 1, 5, 2)
        finish(0, 1, 7, 3)
        z_q[1, 1] = quantise(interleave_z(1, 1), "z_1_1", at=AFTER_GATE)
        finish(0, 2, 6, 4)
        finish(1, 0, 5, 2)
        finish(1, 1, 0, 1)
        finish(1, 2, 7, 3)
